import numpy as np, ml_dtypes
CORES = [9,25,41,57]
N = 4
BF = ml_dtypes.bfloat16
def gentries(a):
    return np.ascontiguousarray(a.reshape(8, 16, -1).transpose(0, 2, 1)).reshape(8, -1)
def gtable(e):
    e = np.asarray(e); return np.ascontiguousarray(e.reshape(8, -1, 16).transpose(0, 2, 1)).reshape(128, -1).astype(np.int32)
W, S, M, K, R, D = 4096, 4, 1024, 1024, 3, 1
def places(rng):
    o = np.argsort(rng.random((N, 8, W)), axis=-1)[..., :2 * K]
    return np.array(o[..., :K]), np.array(o[..., K:])
def keys(rng):
    x = np.array(np.argsort(rng.random((N, 8, M)), axis=-1)[..., :K]).astype(np.int64)
    o = 2 * rng.integers(0, M // 2, (N, 8, 1)) + 1; e = rng.integers(0, M // 2, (N, 8, 1)); f = rng.integers(0, M // 2, (N, 8, 1))
    return (o + 2 * e * x + 2 * f * x * x) & (M - 1), x
def pack(m, th, A, B, a, b):
    return {"mk": np.ascontiguousarray(m.reshape(N, 128, W)).astype(np.float32).astype(BF), "th": np.ascontiguousarray(np.repeat(th, 16, axis=1).reshape(N, 128, 1)).astype(np.int32),
            "la": np.stack([gtable(v) for v in A]), "lb": np.stack([gtable(v) for v in B]), "ka": np.stack([gtable(v) for v in a]), "kb": np.stack([gtable(v) for v in b])}
def setup_inputs(rng):
    A, B = places(rng); a, b = keys(rng)
    return pack(rng.integers(0, 16, (N, 8, 16, W)), rng.integers(112, 160, (N, 8)), A, B, a, b)
def far(rng, back):
    G = max(g for g in range(1, W - 2 * K + 1) if g + max(0, (g - 1 + S // 2) // S - (M - K)) <= W - 2 * K)
    h = (G - 1 + S // 2) // S; mv = max(0, h - (M - K))
    x = int(rng.integers(1, K // 2))
    while ((W - 1 - S // 2 if back else 0) - (K - mv + x + G - 2)) % S: x += 1
    u = K - 1 - mv + x; base = u + G + K - x; e = u + G - 1; e = W - 1 - e if back else e; c = e // S
    near = c + np.arange(1, h + 1) * (1 if back else -1); rest = np.setdiff1d(np.arange(M), np.append(near, c))
    o = [rng.permutation(K) for q in range(N)]
    s = np.stack([np.concatenate([np.array([c]), rng.permutation(near)[:mv], rng.permutation(rest)[:K - 1 - mv]])[o[q]] for q in range(N)])
    A, B = np.zeros((N, K), np.int64), np.zeros((N, K), np.int64)
    for r in range(N):
        P = np.concatenate([np.array([u - 1]), base + 2 + 2 * np.arange(mv), rng.permutation(np.append(np.arange(x, u - 1), base))])
        Q = rng.permutation(np.concatenate([np.arange(x), u + G + np.arange(K - x)]))
        if back: A[r], B[r] = W - 1 - Q, W - 1 - P[o[(r - D) % N]]
        else: A[r], B[r] = P[o[r]], Q
    return A, B, s
def setup_inputs_full(rng):
    A, B = places(rng); a, b = keys(rng); th = np.full((N, 8), 241); lone = []
    for q in range(N):
        for g in range(6):
            k = (g + q) & 7; o = rng.permutation(2 * K)
            if k == 0:
                i = int(np.argmax(o)); o[i], o[K] = int(o[K]), int(o[i]); A[q, g], B[q, g] = o[:K], o[K:]
            elif k == 1:
                i = int(np.argmin(o)); o[i], o[0] = int(o[0]), int(o[i]); A[q, g], B[q, g] = W - 2 * K + o[:K], W - 2 * K + o[K:]
            elif k == 2:
                A[q, g] = rng.permutation(K); B[q, g] = W - K + rng.permutation(K)
            elif k == 3:
                A[q, g] = W - K + rng.permutation(K); B[q, g] = rng.permutation(K); j = int(rng.integers(0, 16))
                if q % 3 < 2: th[q, g] = 240; lone.append((q, g, K + j if q % 3 == 0 else W - 1 - K - j))
            elif k == 4:
                A[q, g] = S * rng.permutation(M)[:K]; B[q, g] = S * rng.permutation(M)[:K] + S // 2
            elif k == 5:
                A[q, g] = 2 * rng.permutation(K); B[q, g] = 2 * rng.permutation(K) + 1; th[q, g] = rng.integers(112, 160)
            else:
                p = 1 + rng.permutation(W - 2)[:2 * K]; A[q, g], B[q, g] = p[:K], p[K:]; i = rng.integers(0, K); j = rng.integers(0, K)
                A[q, g, i] = (W - 1, 0)[k - 6]; B[q, g, j] = (0, W - 1)[k - 6]
    for g in (6, 7):
        A[:, g], B[:, g], s = far(rng, g == 7)
        a[:, g] = 2 * rng.integers(0, M // 2, (N, 1)) + 1; b[:, g] = (s - 2 * a[:, g]) & (M - 1)
    m = rng.integers(0, 16, (N, 8, 16, W))
    m = np.where((rng.random((N, 8, 1, W)) < 0.25) & (th[:, :, None, None] == 241), 15, m)
    for q, g, w in lone: m[q, g, :, w] = 15
    return pack(m, th, A, B, a, b)
def setup_inputs_sites(rng):
    A, B = places(rng); a, b = keys(rng); th = np.tile(np.array([130, 1, 1, 1, 1, 240, 1, 1]), (N, 1)); t = np.arange(K)
    a[:, 0] = 1; b[:, 0] = t; a[:, 1] = M - 1; b[:, 1] = M - 1 - t
    a[:, 4] = 2 * rng.integers(0, M // 2, (N, 1)) + 1
    F = 1 << ((W - 1).bit_length() - 1); L = W - F
    f1 = rng.permutation(np.arange(-(-F // S), (F + L // 2 - 8) // S, 2))[:16]; f2 = rng.permutation(np.arange(L // 2 // S + 8, (L - 16) // S, 2))[:16]
    pl = np.concatenate([f1, f2]); n = len(pl); rest = np.setdiff1d(np.arange(M), pl); o4 = [rng.permutation(K) for q in range(N)]
    pa = np.concatenate([S * f1 - F, S * f2 - 1]); pb = np.concatenate([S * f1 + S // 2 + 1, S * f2 + S // 2 + F])
    other = np.setdiff1d(np.arange(W), np.concatenate([pa, pb, S * pl, S * pl + S // 2]))
    for q in range(N):
        b[q, 4] = (np.concatenate([pl, rng.permutation(rest)[:K - n]])[o4[q]] - 2 * a[q, 4]) & (M - 1)
        w = rng.permutation(other)
        A[q, 4] = np.concatenate([pa, w[:K - n]])[o4[q]]; B[q, 4] = np.concatenate([pb, w[K - n:2 * (K - n)]])[o4[(q - D) % N]]
    lim = 3 * (M - K) // 2; v = np.arange(M); v = v[(v % 3 == 1) | (v >= lim)]
    a[:, 5] = 3 * (2 * rng.integers(0, 4, (N, 1)) + 1); b[:, 5] = (np.stack([rng.permutation(v) for q in range(N)]) - 2 * a[:, 5]) & (M - 1)
    s = (a * 2 + b) & (M - 1); z = np.roll(s, D, axis=0)
    A[:, 2] = S * s[:, 2]; B[:, 2] = S * z[:, 2] + S // 2
    A[:, 3] = S * np.roll(s[:, 3], -1, axis=-1); B[:, 3] = S * np.roll(z[:, 3], -1, axis=-1) + S // 2
    s5, z5 = s[:, 5], z[:, 5]; go = (s5 % 3 == 1) & ((s5 < lim) | (S > 2)); kind = rng.integers(0, 3, (N, K))
    ga = (go & (kind != 2)).astype(np.int64); gb = np.roll(go & (kind != 1), D, axis=0).astype(np.int64)
    A[:, 5] = np.where(s5 % 3 == 2, S * s5 + S // 2, S * s5 - ga); B[:, 5] = np.where(z5 % 3 == 2, S * z5, S * z5 + S // 2 + gb)
    for q in range(N):
        for g in (6, 7):
            w = rng.random(W); w[S * s[q, g]] += 8 - g; w[S * z[q, g] + S // 2] += g - 5
            o = rng.permutation(np.argsort(w)[:2 * K]); A[q, g], B[q, g] = o[:K], o[K:]
    m = rng.integers(0, 16, (N, 8, 16, W)); m[:, 5] = np.where(taken(A, B)[:, 5][:, None, :], m[:, 5], 15)
    return pack(m, th, A, B, a, b)
def setup_inputs_spread(rng):
    A, B = places(rng); a, b = keys(rng)
    m = np.floor(rng.random((N, 8, 16, W)) * (rng.integers(0, 16, (N, 8, 1, W)) + 1)).astype(np.int64)
    return pack(m, rng.integers(1, 242, (N, 8)), A, B, a, b)
def setup_inputs_stall(rng):
    A, B = places(rng); a, b = keys(rng); th = np.full((N, 8), 1); th[((np.arange(N) // np.gcd(D, N)) & 1) == 1, 1::2] = 241
    m = rng.integers(0, 16, (N, 8, 16, W)) * (rng.random((N, 8, 1, W)) > 0.125)
    return pack(m, th, A, B, a, b)
def setup_inputs_ties(rng):
    A, B = places(rng); a, b = keys(rng); th = rng.integers(20, 220, (N, 8))
    T = th[:, :, None] + rng.choice(np.array([-2, -1, -1, -1, 0, 1]), (N, 8, W)); q = T // 16
    m = q[:, :, None, :] + (np.argsort(rng.random((N, 8, 16, W), dtype=np.float32), axis=2) < (T - 16 * q)[:, :, None, :])
    lo, hi = m[:, :, :8], m[:, :, 8:]; d = np.floor(rng.random(lo.shape) * (np.minimum(lo, 15 - hi) + 1)).astype(np.int64)
    return pack(np.concatenate([lo - d, hi + d], axis=2), th, A, B, a, b)
def check_inputs(d):
    bad = []
    x = d["mk"].astype(np.float32)
    if not np.all((x >= 0) & (x <= 15) & (x == np.floor(x))): bad.append("marks")
    for k, lo, hi in (("th", 1, 241), ("la", 0, W - 1), ("lb", 0, W - 1), ("ka", 1, M - 1), ("kb", 0, M - 1)):
        if np.min(d[k]) < lo or np.max(d[k]) > hi: bad.append("range of " + k)
    h = d["th"].reshape(N, 8, 16)
    if np.any(h != h[:, :, :1]): bad.append("th alike in a group")
    if np.any((d["ka"] & 1) == 0): bad.append("odd keys")
    A, B, a, b = [np.stack([gentries(v) for v in d[k]]).astype(np.int64) for k in ("la", "lb", "ka", "kb")]
    if np.any(np.diff(np.sort(np.concatenate([A, B], axis=2), axis=-1), axis=-1) == 0): bad.append("different places")
    for c in range(2, R + 1):
        if np.any(np.diff(np.sort((a * c + b) & (M - 1), axis=-1), axis=-1) == 0): bad.append("different sites in step " + str(c))
    return bad
def taken(A, B):
    o = np.zeros((N, 8, W), bool)
    np.put_along_axis(o, A, True, 2); np.put_along_axis(o, B, True, 2)
    return o
def reference(mk, th, la, lb, ka, kb):
    m = mk.astype(np.float32).astype(np.int64).reshape(N, 8, 16, W); t = th.astype(np.int64).reshape(N, 8, 16)[:, :, :1]
    A, B, a, b = [np.stack([gentries(v) for v in w]).astype(np.int64) for w in (la, lb, ka, kb)]
    at = np.arange(W); still = np.zeros((N, 8, K), bool)
    for c in range(1, R + 1):
        A0, B0 = A, B; held = taken(A, B)
        s = (a * c + b) & (M - 1); sa = S * s; sb = S * np.roll(s, D, axis=0) + S // 2
        A = np.where(still & ~np.take_along_axis(held, sa, 2), sa, A)
        B = np.where(np.roll(still, D, axis=0) & ~np.take_along_axis(held, sb, 2), sb, B)
        bar = np.add.reduce(m, axis=2) >= t
        up = np.maximum.accumulate(np.where(bar | taken(A, B), at + 1, 0), axis=2)
        up = np.concatenate([np.zeros((N, 8, 1), np.int64), up[..., :-1]], axis=2)
        A = np.take_along_axis(up, A, 2)
        dn = np.minimum.accumulate(np.where(bar | taken(A, B), at - 1, W - 1)[..., ::-1], axis=2)[..., ::-1]
        dn = np.concatenate([dn[..., 1:], np.full((N, 8, 1), W - 1)], axis=2)
        B = np.take_along_axis(dn, B, 2)
        ia, ib = A[:, :, None, :], B[:, :, None, :]
        va = np.take_along_axis(m, ia, 3); vb = np.take_along_axis(m, ib, 3)
        np.put_along_axis(m, ia, (va + np.roll(vb, -D, axis=0) + 1) & 15, 3)
        np.put_along_axis(m, ib, (vb + np.roll(va, D, axis=0) + 1) & 15, 3)
        still = (A == A0) & np.roll(B == B0, -D, axis=0)
    return {"ym": m.reshape(N, 128, W).astype(np.float32).astype(BF), "ya": np.stack([gtable(v) for v in A]).astype(np.float32), "yb": np.stack([gtable(v) for v in B]).astype(np.float32)}

@@ -1,0 +1,492 @@
+from concourse.bass import DstId, RemoteDMATransfer
+from concourse.mybir import AluOpType as OP, AxisListType as AX, ActivationFunctionType as AF
+
+F32, BF, I32, U16, F16 = "float32", "bfloat16", "int32", "uint16", "float16"
+STEPS = 3
+MO = 3072
+BIG = float(2 ** 26)
+LEG = 256 * BIG
+PITCH = 4096.0
+BLOCK = PITCH * 256
+ROUND = float(3 * 2 ** 34)
+WHOLE = float(3 * 2 ** 22)
+
+SCRATCH = {}
+for _d, _l in (
+    (I32, "lp:128 kk:128 thi:4 pcol:1 ci:5 ki:128 ks:129 kb0:129 kb1:129 q1:128 qa:128 qb:128 fy:128 fz:128"),
+    (F32, "thn:1 zero:256 winl:4096 winr:4096 pay:1024 cf:8 jrow:16 nrow:256 grow:128 drow:128 dlrow:32 v16:16 ef:16 bof:128 "
+          "idf:128 ca:32 cb:32 cc:34 dd:34 neg:256 bias:8 kf0:129 kf1:129 km:385 kl:384 sp:256 pw:256 lid:256 rid:256 uu:256 "
+          "vf:256 vb:256 s1f:256 s1b:256 gb:257 tf:257 ta:257 lq:257 rq:256 zq:256 tbr:256 ns:257 nl:257 ea:256 pt:256 "
+          "dup:512 tr:512 p0:128 p1:128 p2:128 p3:128 sa:128"),
+    (BF, "eb:16 id1:128 idq:128 idb:128 idn:128 pk:256 wd:144 c2:128 ones:512 st0:7168 st1:7168 st2:7168 outm:4096 zz:256 "
+         "ee:256 msk:2048 hh:1024 gq:1024 ff:2048 sr:256 fr:2048 zs1:1024 zs2:1024 zs3:1024 lm1:1024 lm2:1024 lm3:1024 "
+         "fs1:128 fs2:128 lf1:128 lf2:128"),
+    (F16, "wh:144 yp:2048"),
+    (U16, "cl:16 dl:32 l16:128 so:256 ptr:256 lo16:128 hi16:128 p16:128"),
+):
+    for _e in _l.split():
+        SCRATCH[_e.split(":")[0]] = ("sbuf", [128, int(_e.split(":")[1])], _d)
+for _b in range(8):
+    SCRATCH["ps%d" % _b] = ("psum", [128, 512], F32)
+
+NDMA = 34
+SEMAPHORES = ["eV", "eA", "eP", "eG"] + ["d%d" % _k for _k in range(NDMA)] + ["ak", "sk"] \
+    + ["%s%d" % (_s, _c) for _s in ("al", "ar", "sl", "sr", "af", "sf") for _c in range(1, 4)]
+
+
+def rank_program(g, core, T, topo):
+    rank = T.rank_of(core)
+    if rank is None:
+        return
+    n_r = len(T.cores)
+    nxt, prv = T.cores[(rank + 1) % n_r], T.cores[(rank - 1) % n_r]
+    Q = {"V": g.vector, "A": g.scalar, "P": g.tensor, "G": g, "S": g.sync}
+    cnt = {"eV": 0, "eA": 0, "eP": 0, "eG": 0}
+    known = {q: {} for q in Q}
+    recs = {}
+    total = {}
+    ndma = [0]
+
+    def R(name, a=0, b=None, st=1):
+        b = SCRATCH[name][1][1] if b is None else b
+        return (T[name][:, a:b:st] if st != 1 else T[name][:, a:b], name, a, b)
+
+    def REV(name, n):
+        return (T[name][:, n - 1::-1], name, 0, n)
+
+    def IND(win, off):
+        return (win[0].indirect(off[0]), win[1], win[2], win[3], off)
+
+    def order(q, reads, writes):
+        need = {}
+        for kind, ops in (("r", reads), ("w", writes)):
+            for o in ops:
+                ps = o[1].startswith("ps")
+                for (lo, hi, k, sem, c, qq) in recs.get(o[1], []):
+                    meet = lo < o[3] and o[2] < hi and (kind == "w" or k == "w")
+                    if (ps and qq != q) or (meet and not (ps and q == "P")):
+                        need[sem] = max(need.get(sem, 0), c)
+        for sem in sorted(need):
+            if known[q].get(sem, 0) < need[sem]:
+                Q[q].wait_ge(T.sem[sem], need[sem])
+                known[q][sem] = need[sem]
+
+    def note(q, reads, writes, sem, c):
+        total[sem] = c
+        for o in writes:
+            keep = [r for r in recs.get(o[1], []) if not (o[2] <= r[0] and r[1] <= o[3])]
+            recs[o[1]] = keep + [(o[2], o[3], "w", sem, c, q)]
+        for o in reads:
+            keep = [r for r in recs.get(o[1], []) if not (r[2] == "r" and r[3] == sem and o[2] <= r[0] and r[1] <= o[3])]
+            recs[o[1]] = keep + [(o[2], o[3], "r", sem, c, q)]
+
+    def run(q, ins, outs, fn):
+        reads = [o for o in ins if isinstance(o, tuple)] + [o[4] for o in ins + outs if isinstance(o, tuple) and len(o) == 5]
+        order(q, reads, outs)
+        sem = "e" + q
+        cnt[sem] += 1
+        fn().then_inc(T.sem[sem], 1)
+        note(q, reads, outs, sem, cnt[sem])
+
+    def ap(o):
+        return o[0] if isinstance(o, tuple) else o
+
+    def cp(out, a):
+        run("V", [a], [out], lambda: g.vector.tensor_copy(out[0], a[0]))
+
+    def tt(out, a, b, op):
+        run("V", [a, b], [out], lambda: g.vector.tensor_tensor(out[0], a[0], b[0], op))
+
+    def ts(out, a, s1, op0, s2=None, op1=None):
+        if op1 is None:
+            run("V", [a, s1], [out], lambda: g.vector.tensor_scalar(out[0], a[0], ap(s1), None, op0))
+        else:
+            run("V", [a, s1, s2], [out], lambda: g.vector.tensor_scalar(out[0], a[0], ap(s1), ap(s2), op0, op1))
+
+    def fill(out, v):
+        run("V", [], [out], lambda: g.vector.memset(out[0], v))
+
+    def scan(out, d1, init):
+        d0 = R("neg")
+        run("V", [d0, d1, init], [out], lambda: g.vector.tensor_tensor_scan(out[0], d0[0], d1[0], ap(init), OP.add, OP.max))
+
+    def red(out, a):
+        run("V", [a], [out], lambda: g.vector.tensor_reduce(out[0], a[0], AX.X, OP.max))
+
+    def act(out, a, func=AF.Identity, bias=None, scale=None):
+        kw = {}
+        if bias is not None:
+            kw["bias"] = ap(bias)
+        if scale is not None:
+            kw["scale"] = ap(scale)
+        run("A", [a, bias, scale], [out], lambda: g.scalar.activation(out[0], a[0], func, **kw))
+
+    def mm(out, lhs, rhs, start, stop):
+        run("P", [lhs, rhs], [out], lambda: g.tensor.matmul(out[0], lhs[0], rhs[0], start, stop))
+
+    def iota(out, pattern, base, cm, flt=True):
+        if flt:
+            run("G", [], [out], lambda: g.iota(out[0], pattern, base, cm, allow_small_or_imprecise_dtypes=True))
+        else:
+            run("G", [], [out], lambda: g.iota(out[0], pattern, base, cm))
+
+    def dma(q, out, a):
+        reads = [a] if isinstance(a, tuple) else []
+        writes = [out] if isinstance(out, tuple) else []
+        order(q, reads, writes)
+        sem = "d%d" % ndma[0]
+        ndma[0] += 1
+        Q[q].dma_start(ap(out), ap(a)).then_inc(T.sem[sem], 16)
+        note(q, reads, writes, sem, 16)
+
+    def bits(es):
+        m = 0
+        for e in es:
+            m |= 1 << e
+        return m
+
+    def send(dst, src, land, arrive, sent):
+        es = topo.engines(core, dst)
+        rid, pid, _ = topo.addr(dst)
+        order("G", [src], [])
+        g.remote_dma(land[0], src[0], T.sem[arrive], T.sem[sent], pid, rid, bits(es))
+        note("G", [src], [], sent, len(es))
+        note("X", [], [land], arrive, len(es))
+
+    def exchange(src, land, w, arrive, sent):
+        en, ep = topo.engines(core, nxt), topo.engines(core, prv)
+        h = len(en) // 2
+        order("G", [R(src)], [])
+        tr = []
+        for dst, es, a, b in ((nxt, en[:h], 0, w), (prv, ep[h:2 * h], w, 0)):
+            rid, pid, _ = topo.addr(dst)
+            tr.append(RemoteDMATransfer(dst_ids=[DstId(rid=rid, pnc=pid)], dma_engine_mask=bits(es), remote_sem=T.sem[arrive],
+                                        src=T[src][:, a:a + w], dst=T[land][:, b:b + w]))
+        g.remote_dma_fused(tr, local_sem=T.sem[sent])
+        note("G", [R(src)], [], sent, 2 * h)
+        note("X", [], [R(land)], arrive, 2 * h)
+
+    def rows(name):
+        return (T[name][0:128:16, :], name, 0, SCRATCH[name][1][1])
+
+    def pick(bank, c0, src, a, n, sel):
+        for i in range(16):
+            mm(R(bank, c0, c0 + n), R(sel, 15 - i, 143 - i), R(src, a + i, a + 16 * n, 16), i == 0, i == 15)
+
+    def sums(src, blocks, first):
+        for k, i in enumerate(blocks):
+            mm(R("ps5", 0, 256), R("wd", 15 - i, 143 - i), R(src, MO + 256 * i, MO + 256 * (i + 1)),
+               first and k == 0, not first and k == len(blocks) - 1)
+
+    def taken(first):
+        mm(R("ps5", 0, 256), R("idb"), R("zz"), first, False)
+        mm(R("ps5", 0, 256), R("idf"), R("lid"), False, False)
+        mm(R("ps5", 0, 256), R("idf"), R("rid"), False, not first)
+
+    def clear():
+        dma("S", rows("winl"), R("zero"))
+        dma("S", rows("winr"), R("zero"))
+
+    def scatter_left():
+        act(IND(R("winl"), R("l16", 0, 64)), R("pay"), AF.Silu)
+
+    def scatter_right():
+        ts(IND(R("winr"), R("l16", 64, 128)), R("pay"), -1.0, OP.mult, 2048.0, OP.add)
+        dma("S", R("lid"), rows("winl"))
+        dma("S", R("rid"), rows("winr"))
+
+    def halves(src):
+        ts(R("qb"), src, 8, OP.arith_shift_right)
+        ts(R("qa"), src, 255, OP.bitwise_and)
+        cp(R("hi16"), R("qb"))
+        cp(R("lo16"), R("qa"))
+
+    def masks():
+        act(R("msk", 0, 1024), IND(R("eb"), R("hi16", 0, 64)), scale=1.0 / PITCH)
+        act(R("msk", 1024, 2048), IND(R("eb"), R("hi16", 64, 128)), scale=-1.0 / PITCH)
+
+    store = ["st0", "st1", "st2"]
+    pb = R("ps7", 256, 512)
+
+    dma("S", R("lp", 0, 64), T.la[:])
+    dma("A", R("lp", 64, 128), T.lb[:])
+    fill(R("zero"), 0.0)
+    clear()
+    dma("A", R("kk", 0, 64), T.ka[:])
+    dma("A", R("kk", 64, 128), T.kb[:])
+    dma("A", R("thi", 0, 1), T.th[:])
+    for k in range(4):
+        dma("S", R("st0", MO + 1024 * k, MO + 1024 * (k + 1)), T.mk[:, 1024 * k:1024 * (k + 1)])
+
+    iota(R("pcol"), [[0, 1]], 0, 1, False)
+    iota(R("jrow"), [[1, 16]], 0, 0)
+    iota(R("pay"), [[-1, 1024]], 2047, 0)
+    iota(R("grow"), [[1, 8], [0, 16]], 0, 0)
+    iota(R("drow"), [[1, 128]], 0, -1)
+    iota(R("nrow"), [[1, 256]], 1025, 0)
+    iota(R("dlrow"), [[16, 16], [0, 2]], 0, 0)
+    for s in store:
+        iota(R(s, 1024, 2048), [[0, 1024]], 0, 0)
+    iota(R("ones"), [[0, 512]], 1, 0)
+
+    for k, v in enumerate((ROUND, -ROUND, 2048.0, 1.0)):
+        fill(R("bias", k, k + 1), v)
+    act(R("bias", 4, 5), R("bias", 2, 3), AF.Silu)
+    fill(R("wd"), 0.0)
+    fill(R("wh"), 0.0)
+    fill(R("neg"), -PITCH)
+    fill(R("dd"), 0.0)
+    fill(R("c2"), 1.0)
+    for k, (v, op) in enumerate(((15, OP.bitwise_and), (4, OP.arith_shift_right), (16, OP.bitwise_and), (7, OP.bitwise_and), (8, OP.bitwise_and))):
+        ts(R("ci", k, k + 1), R("pcol"), v, op)
+    fill((T.c2[0:1, :], "c2", 0, 128), 2560.0)
+    cp(R("cf", 0, 5), R("ci"))
+    icol, gcol = R("cf", 0, 1), R("cf", 1, 2)
+    ts(R("v16"), R("jrow"), -1.0, OP.mult, icol, OP.add)
+    ts(R("cc", 16, 17), icol, -BLOCK / LEG, OP.mult)
+    ts(R("cc", 33, 34), icol, -15.0, OP.add, BLOCK / LEG, OP.mult)
+    ts(R("ks", 128, 129), R("cf", 3, 4), -64.0, OP.mult, 448.0, OP.add)
+    ts(R("ef"), R("v16"), 0.0, OP.is_equal)
+    ts(R("eb"), R("v16"), 0.0, OP.is_equal)
+    ts(R("ca", 0, 16), R("v16"), -1.0, OP.add, -BLOCK / LEG, OP.mult)
+    ts(R("cb", 0, 16), R("v16"), -0.5, OP.add, 8 * BIG / LEG, OP.mult)
+    ts(R("ca", 16, 32), R("v16"), 1.0, OP.add, BLOCK / LEG, OP.mult)
+    ts(R("cb", 16, 32), R("v16"), 0.5, OP.add, -8 * BIG / LEG, OP.mult)
+    tt(R("cc", 0, 16), R("ca", 0, 16), R("cb", 0, 16), OP.min)
+    tt(R("cc", 17, 33), R("ca", 16, 32), R("cb", 16, 32), OP.min)
+    cp(R("l16"), R("lp"))
+    scatter_left()
+    ts(R("bof"), R("grow"), gcol, OP.is_equal)
+    halves(R("lp"))
+    for c in (2, 3):
+        ts(R("ki", 64 * c - 128, 64 * c - 64), R("kk", 0, 64), float(c), OP.mult)
+    ts(R("wd", 15, 143, 16), R("bof", 0, 128, 16), BIG, OP.mult)
+    for c in (2, 3):
+        tt(R("ki", 64 * c - 128, 64 * c - 64), R("ki", 64 * c - 128, 64 * c - 64), R("kk", 64, 128), OP.add)
+    scatter_right()
+    clear()
+    masks()
+    ts(R("thn"), R("thi", 0, 1), -1.0, OP.mult)
+    ts(R("idb"), R("drow"), 0.0, OP.is_equal, BIG, OP.mult)
+    ts(R("idf"), R("drow"), 0.0, OP.is_equal, LEG, OP.mult)
+    ts(R("zz"), R("zero"), R("thn"), OP.add)
+    ts(R("ks", 0, 128), R("ki"), 1023, OP.bitwise_and)
+    cp(R("wh", 15, 143, 16), R("bof", 0, 128, 16))
+    cp(R("p0"), R("lp"))
+    ts(R("kb0"), R("ks"), 64, OP.bitwise_and)
+    ts(R("kb1"), R("ks"), 128, OP.bitwise_and)
+    ts(R("kf0"), R("kb0"), -1.0 / 64, OP.mult, 2.0, OP.add)
+    ts(R("kf1"), R("kb1"), -3.0 / 128, OP.mult, 4.0, OP.add)
+    ts(R("kb0"), R("ks"), 256, OP.bitwise_and)
+    tt(R("kf0"), R("kf0"), R("kf1"), OP.mult)
+    ts(R("kb1"), R("ks"), 63, OP.bitwise_and)
+    ts(R("kf1"), R("kb0"), -15.0 / 256 / (16 * BIG), OP.mult, 1.0 / BIG, OP.add)
+    ts(R("ki"), R("ks", 0, 128), 512, OP.bitwise_and)
+    tt(R("km", 256, 385), R("kf0"), R("kf1"), OP.mult)
+    cp(R("km", 0, 128), R("ks", 0, 128))
+    ts(R("kf0"), R("kb1"), 2.0, OP.mult)
+    ts(R("kf1", 0, 128), R("ki"), 0.25, OP.mult)
+    tt(R("km", 128, 256), R("kf0", 0, 128), R("kf1", 0, 128), OP.add)
+    send(nxt, R("km", 0, 384), R("kl"), "ak", "sk")
+    sums("st0", list(range(16)), True)
+    taken(False)
+
+    def mix_constants():
+        ts(R("id1"), R("drow"), 0.0, OP.is_equal)
+        ts(R("idq"), R("drow"), 0.0, OP.is_equal, 0.0625, OP.mult)
+        ts(R("idn"), R("drow"), 0.0, OP.is_equal, -1.0, OP.mult)
+
+    def map_constants():
+        ts(R("cf", 5, 6), R("cf", 4, 5), 2 * BIG, OP.mult, R("km", 384, 385), OP.mult)
+        ts(R("cf", 7, 8), icol, 256.0, OP.mult)
+        ts(R("cf", 6, 7), R("km", 384, 385), 16 * BIG, OP.mult, R("cf", 5, 6), OP.subtract)
+        ts(R("pk", 128, 256), R("bof"), R("cf", 5, 6), OP.mult)
+        ts(R("pk", 0, 128), R("bof"), R("cf", 6, 7), OP.mult)
+
+    def pointer_constants():
+        ts(pb, R("nrow"), R("cf", 7, 8), OP.add)
+        ts(R("dl"), R("dlrow"), icol, OP.add)
+        ts(R("cf", 7, 8), icol, 32.0, OP.mult, R("cf", 2, 3), OP.add)
+        ts(R("cl"), R("jrow"), R("cf", 7, 8), OP.add)
+
+    def site_tables():
+        for o in (0, 64):
+            cp(R("so", 2 * o, 2 * o + 64), R("km", 128 + o, 192 + o))
+            ts(R("so", 2 * o + 64, 2 * o + 128), R("kl", 128 + o, 192 + o), 1.0, OP.add)
+
+    def site_places(c):
+        o, d = 64 * (c - 2), 128 * (c - 2)
+        act(R("sp", d, d + 64), R("km", o, o + 64), scale=4.0)
+        act(R("sp", d + 64, d + 128), R("kl", o, o + 64), scale=4.0, bias=2.0)
+        act(R("pw", d, d + 64), R("km", 256 + o, 320 + o))
+        act(R("pw", d + 64, d + 128), R("kl", 256 + o, 320 + o))
+
+    for c in range(1, STEPS + 1):
+        cur = store[c - 1]
+        pstart = "p%d" % (c - 1)
+        pend = "p%d" % c
+        pre = R("p0") if c == 1 else R("q1")
+        more = c < STEPS
+        d = 128 * (c - 1)
+        mm(R("ps6", 0, 34), R("idf"), R("cc"), True, False)
+        tt(R("vf"), R("ps5", 0, 256), R("rid"), OP.min)
+        tt(R("vb"), R("ps5", 0, 256), R("lid"), OP.min)
+        scan(R("s1f"), R("vf"), -BIG)
+        scan(REV("s1b", 256), REV("vb", 256), -BIG)
+        ts(R("dd", 0, 16), R("ef"), R("s1f", 255, 256), OP.mult)
+        ts(R("dd", 17, 33), R("ef"), R("s1b", 0, 1), OP.mult)
+        mm(R("ps6", 0, 34), R("bof"), R("dd"), False, True)
+        if c == 1:
+            map_constants()
+        red(R("gb", 256, 257), R("ps6", 17, 34))
+        red(R("ps2", 0, 1), R("ps6", 0, 17))
+        scan(REV("gb", 256), REV("vb", 256), R("gb", 256, 257))
+        scan(R("ps2", 1, 257), R("vf"), R("ps2", 0, 1))
+        act(R("ta"), R("gb"), bias=R("bias", 0, 1))
+        act(R("ps0", 0, 257), R("ta"), bias=R("bias", 1, 2))
+        act(R("ea"), R("gb", 1, 257), AF.Abs)
+        act(R("ps3", 0, 256), R("ea"), AF.Relu, scale=-4.0, bias=R("bias", 4, 5))
+        ts(R("tf"), R("ps2", 0, 257), ROUND, OP.add, ROUND, OP.subtract)
+        tt(R("yp", 0, 1024), IND(R("tf", 0, 256), R("lo16", 0, 64)), R("msk", 0, 1024), OP.mult)
+        pick("ps7", 0, "yp", 0, 64, "wh")
+        tt(R("lq"), R("gb"), R("ps0", 0, 257), OP.subtract)
+        act(R("zq"), R("lq", 1, 257), AF.Relu, scale=-1.0, bias=R("bias", 3, 4))
+        tt(R("ns"), R("lq"), R("tf"), OP.add)
+        act(R("nl"), R("ns"), AF.Relu)
+        tt(R("tbr"), R("ps0", 1, 257), R("zq"), OP.mult)
+        tt(R("yp", 1024, 2048), IND(R("tbr"), R("lo16", 64, 128)), R("msk", 1024, 2048), OP.mult)
+        pick("ps7", 64, "yp", 1024, 64, "wh")
+        if more:
+            site_places(c + 1)
+        tt(R("rq"), R("ps2", 1, 257), R("tf", 1, 257), OP.subtract)
+        tt(R("ps1", 0, 256), R("ps3", 0, 256), R("nl", 1, 257), OP.max)
+        tt(R(pend), R("ps7", 0, 128), pre, OP.add)
+        cp(R("p16"), R(pend))
+        win = R(cur, MO, MO + 4096)
+        zs, lm = "zs%d" % c, "lm%d" % c
+        for k in range(2):
+            act(R("hh", 512 * k, 512 * (k + 1)), IND(win, R("p16", 64 * k + 32, 64 * k + 64)), scale=16.0)
+        tt(R("ps1", 256, 512), R("ps1", 0, 256), R("rq"), OP.min)
+        if more:
+            tt(R("fs%d" % c), R(pend), R(pstart), OP.is_equal)
+            exchange("fs%d" % c, "lf%d" % c, 64, "af%d" % c, "sf%d" % c)
+        else:
+            dma("S", T.ya[:], R(pend, 0, 64))
+            dma("S", T.yb[:], R(pend, 64, 128))
+        tt(R("uu"), R("ps1", 256, 512), R("nl", 0, 256), OP.subtract)
+        if more:
+            ts(R("ee"), R("uu"), 0.0, OP.is_equal)
+            for h in range(2):
+                mm(R("ps4", 128 * h, 128 * (h + 1)), R("pk", 128 * h, 128 * (h + 1)), R("ee", 0, 256, 2), True, True)
+            act(R("sr"), R("ps4", 0, 256))
+        tt(R(zs, 0, 512), IND(win, R("p16", 0, 32)), R("hh", 0, 512), OP.add)
+        send(nxt, R(zs, 0, 512), R(lm, 512, 1024), "ar%d" % c, "sl%d" % c)
+        if c == 1:
+            site_tables()
+        if more:
+            act(R("fr", 0, 1024), IND(R("sr"), R("so", d, d + 64)))
+            pick("ps4", 0, "fr", 0, 64, "wd")
+            act(R("fr", 1024, 1536), IND(R("sr"), R("so", d + 64, d + 96)))
+        tt(R(zs, 512, 1024), IND(win, R("p16", 64, 96)), R("hh", 512, 1024), OP.add)
+        send(prv, R(zs, 512, 1024), R(lm, 0, 512), "al%d" % c, "sr%d" % c)
+        if c == 1:
+            pointer_constants()
+        if more:
+            cp(R("fr", 1536, 2048), IND(R("sr"), R("so", d + 96, d + 128)))
+            pick("ps4", 64, "fr", 1024, 64, "wd")
+        else:
+            ts(R("ee"), R("uu"), 0.0, OP.is_equal)
+        tt(R("ps6", 256, 512), pb, R("ee"), OP.mult)
+        if more:
+            tt(R("ps6", 0, 128), R("sp", d, d + 128), R(pend), OP.subtract)
+        tt(R("pt"), R("ps6", 256, 512), R("uu"), OP.add)
+        act(R("dup"), IND(R("pt"), R("dl")))
+        if c == 1:
+            mix_constants()
+        for b in range(4):
+            k = b // 2
+            bare = more and b % 2 == 0
+            if not bare:
+                mm(R("ps%d" % b), (T.c2[0:2, :], "c2", 0, 128), (T.ones[0:2, :], "ones", 0, 512), True, False)
+            if b % 2 == 0:
+                mm(R("ps%d" % b), R("id1"), R(zs, 512 * k, 512 * (k + 1)), bare, False)
+            else:
+                mm(R("ps%d" % b), R("idq"), R("hh", 512 * k, 512 * (k + 1)), False, False)
+
+        def pointers():
+            run("V", [R("dup")], [R("tr")], lambda: g.vector.transpose(T.tr[:], T.dup[:]))
+            ts(R("ptr"), IND(R("tr"), R("cl")), WHOLE + 2047.0, OP.add, WHOLE, OP.subtract)
+
+        def partner(b):
+            k = b // 2
+            if b % 2 == 0:
+                mm(R("ps%d" % b), R("id1"), R(lm, 512 * k, 512 * (k + 1)), False, True)
+            else:
+                mm(R("ps%d" % b), R("idq"), R("gq", 512 * k, 512 * (k + 1)), False, True)
+            act(R("ff", 512 * b, 512 * (b + 1)), R("ps%d" % b), bias=2553.5 if more and b % 2 == 0 else -7.5)
+
+        def high(k):
+            ts(R("gq", 512 * k, 512 * (k + 1)), R(lm, 512 * k, 512 * (k + 1)), 2552.5, OP.add)
+
+        def mixed(b):
+            return R(cur, 2048 * (b // 2) + 512 * (b % 2), 2048 * (b // 2) + 512 * (b % 2 + 1))
+
+        def less(b):
+            tt(mixed(b), R("ps%d" % b), R("ff", 512 * b, 512 * (b + 1)), OP.subtract)
+
+        if more:
+            tt(R("sa"), R("fs%d" % c), R("lf%d" % c), OP.mult)
+            tt(R("fy"), R("ps4", 0, 128), R("pw", d, d + 128), OP.mult)
+            tt(R("ps6", 128, 256), R("ps6", 0, 128), R("sa"), OP.mult)
+            ts(R("fz"), R("fy"), 7, OP.arith_shift_right, 1, OP.bitwise_and)
+            tt(R("ps6", 0, 128), R("ps6", 128, 256), R("fz"), OP.mult)
+            tt(R("q1"), R("ps6", 0, 128), R(pend), OP.add)
+            cp(R("l16"), R("q1"))
+            scatter_left()
+            scatter_right()
+            if c < STEPS - 1:
+                clear()
+            twin = {2: "ps4", 0: "ps6"}
+            for b in (2, 0):
+                mm(R(twin[b]), R("id1"), R(zs, 256 * b, 256 * b + 512), True, False)
+            high(1)
+            high(0)
+            for b in (2, 0):
+                partner(b)
+                mm(R(twin[b]), R("id1"), R(lm, 256 * b, 256 * b + 512), False, False)
+            for b in (3, 1):
+                partner(b)
+            for b in (2, 0):
+                mm(R(twin[b]), R("idn"), R("ff", 512 * b, 512 * (b + 1)), False, True)
+                act(mixed(b), R(twin[b]), bias=2561.0)
+            pointers()
+            halves(R("q1"))
+            for b in (3, 1):
+                less(b)
+            taken(True)
+            parts = [("A", 0, 3), ("V", 8, 11), ("A", 3, 5), ("V", 11, 13), ("A", 5, 7), ("V", 13, 15), ("A", 7, 8), ("V", 15, 16)]
+        else:
+            pointers()
+            for k in (1, 0):
+                high(k)
+                partner(2 * k)
+                partner(2 * k + 1)
+                less(2 * k)
+                less(2 * k + 1)
+            parts = [("A", 0, 1), ("V", 8, 9), ("A", 1, 3), ("V", 9, 11), ("A", 3, 6), ("V", 11, 14), ("A", 6, 8), ("V", 14, 16)]
+        dst, o = (store[c], MO) if more else ("outm", 0)
+        for q, a, b in parts:
+            out, src = R(dst, o + 256 * a, o + 256 * b), IND(R(cur), R("ptr", 16 * a, 16 * b))
+            if q == "A":
+                act(out, src)
+            else:
+                cp(out, src)
+            if not more:
+                dma("S", T.ym[:, 256 * a:256 * b], out)
+        if more:
+            sums(dst, [i for q, a, b in parts for i in range(a, b)], False)
+            masks()
+
+    for sem in sorted(total):
+        if known["G"].get(sem, 0) < total[sem]:
+            g.wait_ge(T.sem[sem], total[sem])

@@ -195,10 +195,12 @@ def rank_program(g, core, T, topo):
         dma("S", R("lid"), rows("winl"))
         dma("S", R("rid"), rows("winr"))
 
-    def halves(src):
+    def high_half(src):
         ts(R("qb"), src, 8, OP.arith_shift_right)
-        ts(R("qa"), src, 255, OP.bitwise_and)
         cp(R("hi16"), R("qb"))
+
+    def low_half(src):
+        ts(R("qa"), src, 255, OP.bitwise_and)
         cp(R("lo16"), R("qa"))
 
     def masks():
@@ -257,7 +259,8 @@ def rank_program(g, core, T, topo):
     cp(R("l16"), R("lp"))
     scatter_left()
     ts(R("bof"), R("grow"), gcol, OP.is_equal)
-    halves(R("lp"))
+    high_half(R("lp"))
+    low_half(R("lp"))
     for c in (2, 3):
         ts(R("ki", 64 * c - 128, 64 * c - 64), R("kk", 0, 64), float(c), OP.mult)
     ts(R("wd", 15, 143, 16), R("bof", 0, 128, 16), BIG, OP.mult)
@@ -292,7 +295,6 @@ def rank_program(g, core, T, topo):
     taken(False)
 
     def mix_constants():
-        ts(R("id1"), R("drow"), 0.0, OP.is_equal)
         ts(R("idq"), R("drow"), 0.0, OP.is_equal, 0.0625, OP.mult)
         ts(R("idn"), R("drow"), 0.0, OP.is_equal, -1.0, OP.mult)
 
@@ -302,6 +304,7 @@ def rank_program(g, core, T, topo):
         ts(R("cf", 6, 7), R("km", 384, 385), 16 * BIG, OP.mult, R("cf", 5, 6), OP.subtract)
         ts(R("pk", 128, 256), R("bof"), R("cf", 5, 6), OP.mult)
         ts(R("pk", 0, 128), R("bof"), R("cf", 6, 7), OP.mult)
+        ts(R("id1"), R("drow"), 0.0, OP.is_equal)
 
     def pointer_constants():
         ts(pb, R("nrow"), R("cf", 7, 8), OP.add)
@@ -325,9 +328,11 @@ def rank_program(g, core, T, topo):
         cur = store[c - 1]
         pstart = "p%d" % (c - 1)
         pend = "p%d" % c
-        pre = R("p0") if c == 1 else R("q1")
+        pre = "p0" if c == 1 else "q1"
         more = c < STEPS
         d = 128 * (c - 1)
+        win = R(cur, MO, MO + 4096)
+        zs, lm = "zs%d" % c, "lm%d" % c
         mm(R("ps6", 0, 34), R("idf"), R("cc"), True, False)
         tt(R("vf"), R("ps5", 0, 256), R("rid"), OP.min)
         tt(R("vb"), R("ps5", 0, 256), R("lid"), OP.min)
@@ -338,14 +343,18 @@ def rank_program(g, core, T, topo):
         mm(R("ps6", 0, 34), R("bof"), R("dd"), False, True)
         if c == 1:
             map_constants()
-        red(R("gb", 256, 257), R("ps6", 17, 34))
+        else:
+            low_half(R("q1"))
         red(R("ps2", 0, 1), R("ps6", 0, 17))
-        scan(REV("gb", 256), REV("vb", 256), R("gb", 256, 257))
+        red(R("gb", 256, 257), R("ps6", 17, 34))
         scan(R("ps2", 1, 257), R("vf"), R("ps2", 0, 1))
+        scan(REV("gb", 256), REV("vb", 256), R("gb", 256, 257))
         act(R("ta"), R("gb"), bias=R("bias", 0, 1))
         act(R("ps0", 0, 257), R("ta"), bias=R("bias", 1, 2))
         act(R("ea"), R("gb", 1, 257), AF.Abs)
         act(R("ps3", 0, 256), R("ea"), AF.Relu, scale=-4.0, bias=R("bias", 4, 5))
+        if c == 2:
+            site_places(3)
         ts(R("tf"), R("ps2", 0, 257), ROUND, OP.add, ROUND, OP.subtract)
         tt(R("yp", 0, 1024), IND(R("tf", 0, 256), R("lo16", 0, 64)), R("msk", 0, 1024), OP.mult)
         pick("ps7", 0, "yp", 0, 64, "wh")
@@ -353,49 +362,54 @@ def rank_program(g, core, T, topo):
         act(R("zq"), R("lq", 1, 257), AF.Relu, scale=-1.0, bias=R("bias", 3, 4))
         tt(R("ns"), R("lq"), R("tf"), OP.add)
         act(R("nl"), R("ns"), AF.Relu)
+        tt(R(pend, 0, 64), R("ps7", 0, 64), R(pre, 0, 64), OP.add)
         tt(R("tbr"), R("ps0", 1, 257), R("zq"), OP.mult)
+        cp(R("p16", 0, 64), R(pend, 0, 64))
+        act(R("hh", 0, 512), IND(win, R("p16", 32, 64)), scale=16.0)
+        act(R("gq", 0, 512), IND(win, R("p16", 0, 32)))
         tt(R("yp", 1024, 2048), IND(R("tbr"), R("lo16", 64, 128)), R("msk", 1024, 2048), OP.mult)
         pick("ps7", 64, "yp", 1024, 64, "wh")
-        if more:
-            site_places(c + 1)
+        mm(R("ps5"), R("id1"), R("hh", 0, 512), True, False)
+        mm(R("ps5"), R("id1"), R("gq", 0, 512), False, True)
+        if not more:
+            act(R(zs, 0, 512), R("ps5"))
+            send(nxt, R(zs, 0, 512), R(lm, 512, 1024), "ar%d" % c, "sl%d" % c)
         tt(R("rq"), R("ps2", 1, 257), R("tf", 1, 257), OP.subtract)
         tt(R("ps1", 0, 256), R("ps3", 0, 256), R("nl", 1, 257), OP.max)
-        tt(R(pend), R("ps7", 0, 128), pre, OP.add)
-        cp(R("p16"), R(pend))
-        win = R(cur, MO, MO + 4096)
-        zs, lm = "zs%d" % c, "lm%d" % c
-        for k in range(2):
-            act(R("hh", 512 * k, 512 * (k + 1)), IND(win, R("p16", 64 * k + 32, 64 * k + 64)), scale=16.0)
         tt(R("ps1", 256, 512), R("ps1", 0, 256), R("rq"), OP.min)
+        tt(R(pend, 64, 128), R("ps7", 64, 128), R(pre, 64, 128), OP.add)
+        cp(R("p16", 64, 128), R(pend, 64, 128))
+        for h in range(2):
+            act(R("hh", 512 + 256 * h, 768 + 256 * h), IND(win, R("p16", 96 + 16 * h, 112 + 16 * h)), scale=16.0)
         if more:
+            act(R(zs, 0, 512), R("ps5"))
             tt(R("fs%d" % c), R(pend), R(pstart), OP.is_equal)
             exchange("fs%d" % c, "lf%d" % c, 64, "af%d" % c, "sf%d" % c)
+            send(nxt, R(zs, 0, 512), R(lm, 512, 1024), "ar%d" % c, "sl%d" % c)
         else:
             dma("S", T.ya[:], R(pend, 0, 64))
             dma("S", T.yb[:], R(pend, 64, 128))
         tt(R("uu"), R("ps1", 256, 512), R("nl", 0, 256), OP.subtract)
+        ts(R("ee"), R("uu"), 0.0, OP.is_equal)
         if more:
-            ts(R("ee"), R("uu"), 0.0, OP.is_equal)
             for h in range(2):
                 mm(R("ps4", 128 * h, 128 * (h + 1)), R("pk", 128 * h, 128 * (h + 1)), R("ee", 0, 256, 2), True, True)
             act(R("sr"), R("ps4", 0, 256))
-        tt(R(zs, 0, 512), IND(win, R("p16", 0, 32)), R("hh", 0, 512), OP.add)
-        send(nxt, R(zs, 0, 512), R(lm, 512, 1024), "ar%d" % c, "sl%d" % c)
-        if c == 1:
-            site_tables()
-        if more:
-            act(R("fr", 0, 1024), IND(R("sr"), R("so", d, d + 64)))
-            pick("ps4", 0, "fr", 0, 64, "wd")
+            if c == 1:
+                site_tables()
+                site_places(2)
+            act(R("fr", 0, 640), IND(R("sr"), R("so", d, d + 40)))
             act(R("fr", 1024, 1536), IND(R("sr"), R("so", d + 64, d + 96)))
-        tt(R(zs, 512, 1024), IND(win, R("p16", 64, 96)), R("hh", 512, 1024), OP.add)
+        for h in range(2):
+            tt(R(zs, 512 + 256 * h, 768 + 256 * h), IND(win, R("p16", 64 + 16 * h, 80 + 16 * h)), R("hh", 512 + 256 * h, 768 + 256 * h), OP.add)
         send(prv, R(zs, 512, 1024), R(lm, 0, 512), "al%d" % c, "sr%d" % c)
         if c == 1:
             pointer_constants()
         if more:
+            cp(R("fr", 640, 1024), IND(R("sr"), R("so", d + 40, d + 64)))
+            pick("ps4", 0, "fr", 0, 64, "wd")
             cp(R("fr", 1536, 2048), IND(R("sr"), R("so", d + 96, d + 128)))
             pick("ps4", 64, "fr", 1024, 64, "wd")
-        else:
-            ts(R("ee"), R("uu"), 0.0, OP.is_equal)
         tt(R("ps6", 256, 512), pb, R("ee"), OP.mult)
         if more:
             tt(R("ps6", 0, 128), R("sp", d, d + 128), R(pend), OP.subtract)
@@ -436,8 +450,8 @@ def rank_program(g, core, T, topo):
 
         if more:
             tt(R("sa"), R("fs%d" % c), R("lf%d" % c), OP.mult)
-            tt(R("fy"), R("ps4", 0, 128), R("pw", d, d + 128), OP.mult)
             tt(R("ps6", 128, 256), R("ps6", 0, 128), R("sa"), OP.mult)
+            tt(R("fy"), R("ps4", 0, 128), R("pw", d, d + 128), OP.mult)
             ts(R("fz"), R("fy"), 7, OP.arith_shift_right, 1, OP.bitwise_and)
             tt(R("ps6", 0, 128), R("ps6", 128, 256), R("fz"), OP.mult)
             tt(R("q1"), R("ps6", 0, 128), R(pend), OP.add)
@@ -460,19 +474,23 @@ def rank_program(g, core, T, topo):
                 mm(R(twin[b]), R("idn"), R("ff", 512 * b, 512 * (b + 1)), False, True)
                 act(mixed(b), R(twin[b]), bias=2561.0)
             pointers()
-            halves(R("q1"))
+            high_half(R("q1"))
             for b in (3, 1):
                 less(b)
             taken(True)
             parts = [("A", 0, 3), ("V", 8, 11), ("A", 3, 5), ("V", 11, 13), ("A", 5, 7), ("V", 13, 15), ("A", 7, 8), ("V", 15, 16)]
         else:
             pointers()
-            for k in (1, 0):
-                high(k)
-                partner(2 * k)
-                partner(2 * k + 1)
-                less(2 * k)
-                less(2 * k + 1)
+            high(1)
+            partner(2)
+            partner(3)
+            less(2)
+            partner(0)
+            high(0)
+            less(3)
+            partner(1)
+            less(0)
+            less(1)
             parts = [("A", 0, 1), ("V", 8, 9), ("A", 1, 3), ("V", 9, 11), ("A", 3, 6), ("V", 11, 14), ("A", 6, 8), ("V", 14, 16)]
         dst, o = (store[c], MO) if more else ("outm", 0)
         for q, a, b in parts:

from concourse.bass import DstId, RemoteDMATransfer
from concourse.mybir import AluOpType as OP, AxisListType as AX, ActivationFunctionType as AF

F32, BF, I32, U16, F16 = "float32", "bfloat16", "int32", "uint16", "float16"
STEPS = 3
MO = 3072
BIG = float(2 ** 26)
LEG = 256 * BIG
PITCH = 4096.0
BLOCK = PITCH * 256
ROUND = float(3 * 2 ** 34)
WHOLE = float(3 * 2 ** 22)

SCRATCH = {}
for _d, _l in (
    (I32, "lp:128 kk:128 thi:4 pcol:1 ci:5 ki:128 ks:129 kb0:129 kb1:129 q1:128 qa:128 qb:128 fy:128 fz:128"),
    (F32, "thn:1 zero:256 winl:4096 winr:4096 pay:1024 cf:8 jrow:16 nrow:256 grow:128 drow:128 dlrow:32 v16:16 ef:16 bof:128 "
          "idf:128 ca:32 cb:32 cc:34 dd:34 neg:256 bias:8 kf0:129 kf1:129 km:385 kl:384 sp:256 pw:256 lid:256 rid:256 uu:256 "
          "vf:256 vb:256 s1f:256 s1b:256 gb:257 tf:257 ta:257 lq:257 rq:256 zq:256 tbr:256 ns:257 nl:257 ea:256 pt:256 "
          "dup:512 tr:512 p0:128 p1:128 p2:128 p3:128 sa:128"),
    (BF, "eb:16 id1:128 idq:128 idb:128 idn:128 pk:256 wd:144 c2:128 ones:512 st0:7168 st1:7168 st2:7168 outm:4096 zz:256 "
         "ee:256 msk:2048 hh:1024 gq:1024 ff:2048 sr:256 fr:2048 zs1:1024 zs2:1024 zs3:1024 lm1:1024 lm2:1024 lm3:1024 "
         "fs1:128 fs2:128 lf1:128 lf2:128"),
    (F16, "wh:144 yp:2048"),
    (U16, "cl:16 dl:32 l16:128 so:256 ptr:256 lo16:128 hi16:128 p16:128"),
):
    for _e in _l.split():
        SCRATCH[_e.split(":")[0]] = ("sbuf", [128, int(_e.split(":")[1])], _d)
for _b in range(8):
    SCRATCH["ps%d" % _b] = ("psum", [128, 512], F32)

NDMA = 34
SEMAPHORES = ["eV", "eA", "eP", "eG"] + ["d%d" % _k for _k in range(NDMA)] + ["ak", "sk"] \
    + ["%s%d" % (_s, _c) for _s in ("al", "ar", "sl", "sr", "af", "sf") for _c in range(1, 4)]


def rank_program(g, core, T, topo):
    rank = T.rank_of(core)
    if rank is None:
        return
    n_r = len(T.cores)
    nxt, prv = T.cores[(rank + 1) % n_r], T.cores[(rank - 1) % n_r]
    Q = {"V": g.vector, "A": g.scalar, "P": g.tensor, "G": g, "S": g.sync}
    cnt = {"eV": 0, "eA": 0, "eP": 0, "eG": 0}
    known = {q: {} for q in Q}
    recs = {}
    total = {}
    ndma = [0]

    def R(name, a=0, b=None, st=1):
        b = SCRATCH[name][1][1] if b is None else b
        return (T[name][:, a:b:st] if st != 1 else T[name][:, a:b], name, a, b)

    def REV(name, n):
        return (T[name][:, n - 1::-1], name, 0, n)

    def IND(win, off):
        return (win[0].indirect(off[0]), win[1], win[2], win[3], off)

    def order(q, reads, writes):
        need = {}
        for kind, ops in (("r", reads), ("w", writes)):
            for o in ops:
                ps = o[1].startswith("ps")
                for (lo, hi, k, sem, c, qq) in recs.get(o[1], []):
                    meet = lo < o[3] and o[2] < hi and (kind == "w" or k == "w")
                    if (ps and qq != q) or (meet and not (ps and q == "P")):
                        need[sem] = max(need.get(sem, 0), c)
        for sem in sorted(need):
            if known[q].get(sem, 0) < need[sem]:
                Q[q].wait_ge(T.sem[sem], need[sem])
                known[q][sem] = need[sem]

    def note(q, reads, writes, sem, c):
        total[sem] = c
        for o in writes:
            keep = [r for r in recs.get(o[1], []) if not (o[2] <= r[0] and r[1] <= o[3])]
            recs[o[1]] = keep + [(o[2], o[3], "w", sem, c, q)]
        for o in reads:
            keep = [r for r in recs.get(o[1], []) if not (r[2] == "r" and r[3] == sem and o[2] <= r[0] and r[1] <= o[3])]
            recs[o[1]] = keep + [(o[2], o[3], "r", sem, c, q)]

    def run(q, ins, outs, fn):
        reads = [o for o in ins if isinstance(o, tuple)] + [o[4] for o in ins + outs if isinstance(o, tuple) and len(o) == 5]
        order(q, reads, outs)
        sem = "e" + q
        cnt[sem] += 1
        fn().then_inc(T.sem[sem], 1)
        note(q, reads, outs, sem, cnt[sem])

    def ap(o):
        return o[0] if isinstance(o, tuple) else o

    def cp(out, a):
        run("V", [a], [out], lambda: g.vector.tensor_copy(out[0], a[0]))

    def tt(out, a, b, op):
        run("V", [a, b], [out], lambda: g.vector.tensor_tensor(out[0], a[0], b[0], op))

    def ts(out, a, s1, op0, s2=None, op1=None):
        if op1 is None:
            run("V", [a, s1], [out], lambda: g.vector.tensor_scalar(out[0], a[0], ap(s1), None, op0))
        else:
            run("V", [a, s1, s2], [out], lambda: g.vector.tensor_scalar(out[0], a[0], ap(s1), ap(s2), op0, op1))

    def fill(out, v):
        run("V", [], [out], lambda: g.vector.memset(out[0], v))

    def scan(out, d1, init):
        d0 = R("neg")
        run("V", [d0, d1, init], [out], lambda: g.vector.tensor_tensor_scan(out[0], d0[0], d1[0], ap(init), OP.add, OP.max))

    def red(out, a):
        run("V", [a], [out], lambda: g.vector.tensor_reduce(out[0], a[0], AX.X, OP.max))

    def act(out, a, func=AF.Identity, bias=None, scale=None):
        kw = {}
        if bias is not None:
            kw["bias"] = ap(bias)
        if scale is not None:
            kw["scale"] = ap(scale)
        run("A", [a, bias, scale], [out], lambda: g.scalar.activation(out[0], a[0], func, **kw))

    def mm(out, lhs, rhs, start, stop):
        run("P", [lhs, rhs], [out], lambda: g.tensor.matmul(out[0], lhs[0], rhs[0], start, stop))

    def iota(out, pattern, base, cm, flt=True):
        if flt:
            run("G", [], [out], lambda: g.iota(out[0], pattern, base, cm, allow_small_or_imprecise_dtypes=True))
        else:
            run("G", [], [out], lambda: g.iota(out[0], pattern, base, cm))

    def dma(q, out, a):
        reads = [a] if isinstance(a, tuple) else []
        writes = [out] if isinstance(out, tuple) else []
        order(q, reads, writes)
        sem = "d%d" % ndma[0]
        ndma[0] += 1
        Q[q].dma_start(ap(out), ap(a)).then_inc(T.sem[sem], 16)
        note(q, reads, writes, sem, 16)

    def bits(es):
        m = 0
        for e in es:
            m |= 1 << e
        return m

    def send(dst, src, land, arrive, sent):
        es = topo.engines(core, dst)
        rid, pid, _ = topo.addr(dst)
        order("G", [src], [])
        g.remote_dma(land[0], src[0], T.sem[arrive], T.sem[sent], pid, rid, bits(es))
        note("G", [src], [], sent, len(es))
        note("X", [], [land], arrive, len(es))

    def exchange(src, land, w, arrive, sent):
        en, ep = topo.engines(core, nxt), topo.engines(core, prv)
        h = len(en) // 2
        order("G", [R(src)], [])
        tr = []
        for dst, es, a, b in ((nxt, en[:h], 0, w), (prv, ep[h:2 * h], w, 0)):
            rid, pid, _ = topo.addr(dst)
            tr.append(RemoteDMATransfer(dst_ids=[DstId(rid=rid, pnc=pid)], dma_engine_mask=bits(es), remote_sem=T.sem[arrive],
                                        src=T[src][:, a:a + w], dst=T[land][:, b:b + w]))
        g.remote_dma_fused(tr, local_sem=T.sem[sent])
        note("G", [R(src)], [], sent, 2 * h)
        note("X", [], [R(land)], arrive, 2 * h)

    def rows(name):
        return (T[name][0:128:16, :], name, 0, SCRATCH[name][1][1])

    def pick(bank, c0, src, a, n, sel):
        for i in range(16):
            mm(R(bank, c0, c0 + n), R(sel, 15 - i, 143 - i), R(src, a + i, a + 16 * n, 16), i == 0, i == 15)

    def sums(src, blocks, first):
        for k, i in enumerate(blocks):
            mm(R("ps5", 0, 256), R("wd", 15 - i, 143 - i), R(src, MO + 256 * i, MO + 256 * (i + 1)),
               first and k == 0, not first and k == len(blocks) - 1)

    def taken(first):
        mm(R("ps5", 0, 256), R("idb"), R("zz"), first, False)
        mm(R("ps5", 0, 256), R("idf"), R("lid"), False, False)
        mm(R("ps5", 0, 256), R("idf"), R("rid"), False, not first)

    def clear():
        dma("S", rows("winl"), R("zero"))
        dma("S", rows("winr"), R("zero"))

    def scatter_left():
        act(IND(R("winl"), R("l16", 0, 64)), R("pay"), AF.Silu)

    def scatter_right():
        ts(IND(R("winr"), R("l16", 64, 128)), R("pay"), -1.0, OP.mult, 2048.0, OP.add)
        dma("S", R("lid"), rows("winl"))
        dma("S", R("rid"), rows("winr"))

    def high_half(src):
        ts(R("qb"), src, 8, OP.arith_shift_right)
        cp(R("hi16"), R("qb"))

    def low_half(src):
        ts(R("qa"), src, 255, OP.bitwise_and)
        cp(R("lo16"), R("qa"))

    def masks():
        act(R("msk", 0, 1024), IND(R("eb"), R("hi16", 0, 64)), scale=1.0 / PITCH)
        act(R("msk", 1024, 2048), IND(R("eb"), R("hi16", 64, 128)), scale=-1.0 / PITCH)

    store = ["st0", "st1", "st2"]
    pb = R("ps7", 256, 512)

    dma("S", R("lp", 0, 64), T.la[:])
    dma("A", R("lp", 64, 128), T.lb[:])
    fill(R("zero"), 0.0)
    clear()
    dma("A", R("kk", 0, 64), T.ka[:])
    dma("A", R("kk", 64, 128), T.kb[:])
    dma("A", R("thi", 0, 1), T.th[:])
    for k in range(4):
        dma("S", R("st0", MO + 1024 * k, MO + 1024 * (k + 1)), T.mk[:, 1024 * k:1024 * (k + 1)])

    iota(R("pcol"), [[0, 1]], 0, 1, False)
    iota(R("jrow"), [[1, 16]], 0, 0)
    iota(R("pay"), [[-1, 1024]], 2047, 0)
    iota(R("grow"), [[1, 8], [0, 16]], 0, 0)
    iota(R("drow"), [[1, 128]], 0, -1)
    iota(R("nrow"), [[1, 256]], 1025, 0)
    iota(R("dlrow"), [[16, 16], [0, 2]], 0, 0)
    for s in store:
        iota(R(s, 1024, 2048), [[0, 1024]], 0, 0)
    iota(R("ones"), [[0, 512]], 1, 0)

    for k, v in enumerate((ROUND, -ROUND, 2048.0, 1.0)):
        fill(R("bias", k, k + 1), v)
    act(R("bias", 4, 5), R("bias", 2, 3), AF.Silu)
    fill(R("wd"), 0.0)
    fill(R("wh"), 0.0)
    fill(R("neg"), -PITCH)
    fill(R("dd"), 0.0)
    fill(R("c2"), 1.0)
    for k, (v, op) in enumerate(((15, OP.bitwise_and), (4, OP.arith_shift_right), (16, OP.bitwise_and), (7, OP.bitwise_and), (8, OP.bitwise_and))):
        ts(R("ci", k, k + 1), R("pcol"), v, op)
    fill((T.c2[0:1, :], "c2", 0, 128), 2560.0)
    cp(R("cf", 0, 5), R("ci"))
    icol, gcol = R("cf", 0, 1), R("cf", 1, 2)
    ts(R("v16"), R("jrow"), -1.0, OP.mult, icol, OP.add)
    ts(R("cc", 16, 17), icol, -BLOCK / LEG, OP.mult)
    ts(R("cc", 33, 34), icol, -15.0, OP.add, BLOCK / LEG, OP.mult)
    ts(R("ks", 128, 129), R("cf", 3, 4), -64.0, OP.mult, 448.0, OP.add)
    ts(R("ef"), R("v16"), 0.0, OP.is_equal)
    ts(R("eb"), R("v16"), 0.0, OP.is_equal)
    ts(R("ca", 0, 16), R("v16"), -1.0, OP.add, -BLOCK / LEG, OP.mult)
    ts(R("cb", 0, 16), R("v16"), -0.5, OP.add, 8 * BIG / LEG, OP.mult)
    ts(R("ca", 16, 32), R("v16"), 1.0, OP.add, BLOCK / LEG, OP.mult)
    ts(R("cb", 16, 32), R("v16"), 0.5, OP.add, -8 * BIG / LEG, OP.mult)
    tt(R("cc", 0, 16), R("ca", 0, 16), R("cb", 0, 16), OP.min)
    tt(R("cc", 17, 33), R("ca", 16, 32), R("cb", 16, 32), OP.min)
    cp(R("l16"), R("lp"))
    scatter_left()
    ts(R("bof"), R("grow"), gcol, OP.is_equal)
    high_half(R("lp"))
    low_half(R("lp"))
    for c in (2, 3):
        ts(R("ki", 64 * c - 128, 64 * c - 64), R("kk", 0, 64), float(c), OP.mult)
    ts(R("wd", 15, 143, 16), R("bof", 0, 128, 16), BIG, OP.mult)
    for c in (2, 3):
        tt(R("ki", 64 * c - 128, 64 * c - 64), R("ki", 64 * c - 128, 64 * c - 64), R("kk", 64, 128), OP.add)
    scatter_right()
    clear()
    masks()
    ts(R("thn"), R("thi", 0, 1), -1.0, OP.mult)
    ts(R("idb"), R("drow"), 0.0, OP.is_equal, BIG, OP.mult)
    ts(R("idf"), R("drow"), 0.0, OP.is_equal, LEG, OP.mult)
    ts(R("zz"), R("zero"), R("thn"), OP.add)
    ts(R("ks", 0, 128), R("ki"), 1023, OP.bitwise_and)
    cp(R("wh", 15, 143, 16), R("bof", 0, 128, 16))
    cp(R("p0"), R("lp"))
    ts(R("kb0"), R("ks"), 64, OP.bitwise_and)
    ts(R("kb1"), R("ks"), 128, OP.bitwise_and)
    ts(R("kf0"), R("kb0"), -1.0 / 64, OP.mult, 2.0, OP.add)
    ts(R("kf1"), R("kb1"), -3.0 / 128, OP.mult, 4.0, OP.add)
    ts(R("kb0"), R("ks"), 256, OP.bitwise_and)
    tt(R("kf0"), R("kf0"), R("kf1"), OP.mult)
    ts(R("kb1"), R("ks"), 63, OP.bitwise_and)
    ts(R("kf1"), R("kb0"), -15.0 / 256 / (16 * BIG), OP.mult, 1.0 / BIG, OP.add)
    ts(R("ki"), R("ks", 0, 128), 512, OP.bitwise_and)
    tt(R("km", 256, 385), R("kf0"), R("kf1"), OP.mult)
    cp(R("km", 0, 128), R("ks", 0, 128))
    ts(R("kf0"), R("kb1"), 2.0, OP.mult)
    ts(R("kf1", 0, 128), R("ki"), 0.25, OP.mult)
    tt(R("km", 128, 256), R("kf0", 0, 128), R("kf1", 0, 128), OP.add)
    send(nxt, R("km", 0, 384), R("kl"), "ak", "sk")
    sums("st0", list(range(16)), True)
    taken(False)

    def mix_constants():
        ts(R("idq"), R("drow"), 0.0, OP.is_equal, 0.0625, OP.mult)
        ts(R("idn"), R("drow"), 0.0, OP.is_equal, -1.0, OP.mult)

    def map_constants():
        ts(R("cf", 5, 6), R("cf", 4, 5), 2 * BIG, OP.mult, R("km", 384, 385), OP.mult)
        ts(R("cf", 7, 8), icol, 256.0, OP.mult)
        ts(R("cf", 6, 7), R("km", 384, 385), 16 * BIG, OP.mult, R("cf", 5, 6), OP.subtract)
        ts(R("pk", 128, 256), R("bof"), R("cf", 5, 6), OP.mult)
        ts(R("pk", 0, 128), R("bof"), R("cf", 6, 7), OP.mult)
        ts(R("id1"), R("drow"), 0.0, OP.is_equal)

    def pointer_constants():
        ts(pb, R("nrow"), R("cf", 7, 8), OP.add)
        ts(R("dl"), R("dlrow"), icol, OP.add)
        ts(R("cf", 7, 8), icol, 32.0, OP.mult, R("cf", 2, 3), OP.add)
        ts(R("cl"), R("jrow"), R("cf", 7, 8), OP.add)

    def site_tables():
        for o in (0, 64):
            cp(R("so", 2 * o, 2 * o + 64), R("km", 128 + o, 192 + o))
            ts(R("so", 2 * o + 64, 2 * o + 128), R("kl", 128 + o, 192 + o), 1.0, OP.add)

    def site_places(c):
        o, d = 64 * (c - 2), 128 * (c - 2)
        act(R("sp", d, d + 64), R("km", o, o + 64), scale=4.0)
        act(R("sp", d + 64, d + 128), R("kl", o, o + 64), scale=4.0, bias=2.0)
        act(R("pw", d, d + 64), R("km", 256 + o, 320 + o))
        act(R("pw", d + 64, d + 128), R("kl", 256 + o, 320 + o))

    for c in range(1, STEPS + 1):
        cur = store[c - 1]
        pstart = "p%d" % (c - 1)
        pend = "p%d" % c
        pre = "p0" if c == 1 else "q1"
        more = c < STEPS
        d = 128 * (c - 1)
        win = R(cur, MO, MO + 4096)
        zs, lm = "zs%d" % c, "lm%d" % c
        mm(R("ps6", 0, 34), R("idf"), R("cc"), True, False)
        tt(R("vf"), R("ps5", 0, 256), R("rid"), OP.min)
        tt(R("vb"), R("ps5", 0, 256), R("lid"), OP.min)
        scan(R("s1f"), R("vf"), -BIG)
        scan(REV("s1b", 256), REV("vb", 256), -BIG)
        ts(R("dd", 0, 16), R("ef"), R("s1f", 255, 256), OP.mult)
        ts(R("dd", 17, 33), R("ef"), R("s1b", 0, 1), OP.mult)
        mm(R("ps6", 0, 34), R("bof"), R("dd"), False, True)
        if c == 1:
            map_constants()
        else:
            low_half(R("q1"))
        red(R("ps2", 0, 1), R("ps6", 0, 17))
        red(R("gb", 256, 257), R("ps6", 17, 34))
        scan(R("ps2", 1, 257), R("vf"), R("ps2", 0, 1))
        scan(REV("gb", 256), REV("vb", 256), R("gb", 256, 257))
        act(R("ta"), R("gb"), bias=R("bias", 0, 1))
        act(R("ps0", 0, 257), R("ta"), bias=R("bias", 1, 2))
        act(R("ea"), R("gb", 1, 257), AF.Abs)
        act(R("ps3", 0, 256), R("ea"), AF.Relu, scale=-4.0, bias=R("bias", 4, 5))
        if c == 2:
            site_places(3)
        ts(R("tf"), R("ps2", 0, 257), ROUND, OP.add, ROUND, OP.subtract)
        tt(R("yp", 0, 1024), IND(R("tf", 0, 256), R("lo16", 0, 64)), R("msk", 0, 1024), OP.mult)
        pick("ps7", 0, "yp", 0, 64, "wh")
        tt(R("lq"), R("gb"), R("ps0", 0, 257), OP.subtract)
        act(R("zq"), R("lq", 1, 257), AF.Relu, scale=-1.0, bias=R("bias", 3, 4))
        tt(R("ns"), R("lq"), R("tf"), OP.add)
        act(R("nl"), R("ns"), AF.Relu)
        tt(R(pend, 0, 64), R("ps7", 0, 64), R(pre, 0, 64), OP.add)
        tt(R("tbr"), R("ps0", 1, 257), R("zq"), OP.mult)
        cp(R("p16", 0, 64), R(pend, 0, 64))
        act(R("hh", 0, 512), IND(win, R("p16", 32, 64)), scale=16.0)
        act(R("gq", 0, 512), IND(win, R("p16", 0, 32)))
        tt(R("yp", 1024, 2048), IND(R("tbr"), R("lo16", 64, 128)), R("msk", 1024, 2048), OP.mult)
        pick("ps7", 64, "yp", 1024, 64, "wh")
        mm(R("ps5"), R("id1"), R("hh", 0, 512), True, False)
        mm(R("ps5"), R("id1"), R("gq", 0, 512), False, True)
        if not more:
            act(R(zs, 0, 512), R("ps5"))
            send(nxt, R(zs, 0, 512), R(lm, 512, 1024), "ar%d" % c, "sl%d" % c)
        tt(R("rq"), R("ps2", 1, 257), R("tf", 1, 257), OP.subtract)
        tt(R("ps1", 0, 256), R("ps3", 0, 256), R("nl", 1, 257), OP.max)
        tt(R("ps1", 256, 512), R("ps1", 0, 256), R("rq"), OP.min)
        tt(R(pend, 64, 128), R("ps7", 64, 128), R(pre, 64, 128), OP.add)
        cp(R("p16", 64, 128), R(pend, 64, 128))
        for h in range(2):
            act(R("hh", 512 + 256 * h, 768 + 256 * h), IND(win, R("p16", 96 + 16 * h, 112 + 16 * h)), scale=16.0)
        if more:
            act(R(zs, 0, 512), R("ps5"))
            tt(R("fs%d" % c), R(pend), R(pstart), OP.is_equal)
            exchange("fs%d" % c, "lf%d" % c, 64, "af%d" % c, "sf%d" % c)
            send(nxt, R(zs, 0, 512), R(lm, 512, 1024), "ar%d" % c, "sl%d" % c)
        else:
            dma("S", T.ya[:], R(pend, 0, 64))
            dma("S", T.yb[:], R(pend, 64, 128))
        tt(R("uu"), R("ps1", 256, 512), R("nl", 0, 256), OP.subtract)
        ts(R("ee"), R("uu"), 0.0, OP.is_equal)
        if more:
            for h in range(2):
                mm(R("ps4", 128 * h, 128 * (h + 1)), R("pk", 128 * h, 128 * (h + 1)), R("ee", 0, 256, 2), True, True)
            act(R("sr"), R("ps4", 0, 256))
            if c == 1:
                site_tables()
                site_places(2)
            act(R("fr", 0, 640), IND(R("sr"), R("so", d, d + 40)))
            act(R("fr", 1024, 1536), IND(R("sr"), R("so", d + 64, d + 96)))
        for h in range(2):
            tt(R(zs, 512 + 256 * h, 768 + 256 * h), IND(win, R("p16", 64 + 16 * h, 80 + 16 * h)), R("hh", 512 + 256 * h, 768 + 256 * h), OP.add)
        send(prv, R(zs, 512, 1024), R(lm, 0, 512), "al%d" % c, "sr%d" % c)
        if c == 1:
            pointer_constants()
        if more:
            cp(R("fr", 640, 1024), IND(R("sr"), R("so", d + 40, d + 64)))
            pick("ps4", 0, "fr", 0, 64, "wd")
            cp(R("fr", 1536, 2048), IND(R("sr"), R("so", d + 96, d + 128)))
            pick("ps4", 64, "fr", 1024, 64, "wd")
        tt(R("ps6", 256, 512), pb, R("ee"), OP.mult)
        if more:
            tt(R("ps6", 0, 128), R("sp", d, d + 128), R(pend), OP.subtract)
        tt(R("pt"), R("ps6", 256, 512), R("uu"), OP.add)
        act(R("dup"), IND(R("pt"), R("dl")))
        if c == 1:
            mix_constants()
        for b in range(4):
            k = b // 2
            bare = more and b % 2 == 0
            if not bare:
                mm(R("ps%d" % b), (T.c2[0:2, :], "c2", 0, 128), (T.ones[0:2, :], "ones", 0, 512), True, False)
            if b % 2 == 0:
                mm(R("ps%d" % b), R("id1"), R(zs, 512 * k, 512 * (k + 1)), bare, False)
            else:
                mm(R("ps%d" % b), R("idq"), R("hh", 512 * k, 512 * (k + 1)), False, False)

        def pointers():
            run("V", [R("dup")], [R("tr")], lambda: g.vector.transpose(T.tr[:], T.dup[:]))
            ts(R("ptr"), IND(R("tr"), R("cl")), WHOLE + 2047.0, OP.add, WHOLE, OP.subtract)

        def partner(b):
            k = b // 2
            if b % 2 == 0:
                mm(R("ps%d" % b), R("id1"), R(lm, 512 * k, 512 * (k + 1)), False, True)
            else:
                mm(R("ps%d" % b), R("idq"), R("gq", 512 * k, 512 * (k + 1)), False, True)
            act(R("ff", 512 * b, 512 * (b + 1)), R("ps%d" % b), bias=2553.5 if more and b % 2 == 0 else -7.5)

        def high(k):
            ts(R("gq", 512 * k, 512 * (k + 1)), R(lm, 512 * k, 512 * (k + 1)), 2552.5, OP.add)

        def mixed(b):
            return R(cur, 2048 * (b // 2) + 512 * (b % 2), 2048 * (b // 2) + 512 * (b % 2 + 1))

        def less(b):
            tt(mixed(b), R("ps%d" % b), R("ff", 512 * b, 512 * (b + 1)), OP.subtract)

        if more:
            tt(R("sa"), R("fs%d" % c), R("lf%d" % c), OP.mult)
            tt(R("ps6", 128, 256), R("ps6", 0, 128), R("sa"), OP.mult)
            tt(R("fy"), R("ps4", 0, 128), R("pw", d, d + 128), OP.mult)
            ts(R("fz"), R("fy"), 7, OP.arith_shift_right, 1, OP.bitwise_and)
            tt(R("ps6", 0, 128), R("ps6", 128, 256), R("fz"), OP.mult)
            tt(R("q1"), R("ps6", 0, 128), R(pend), OP.add)
            cp(R("l16"), R("q1"))
            scatter_left()
            scatter_right()
            if c < STEPS - 1:
                clear()
            twin = {2: "ps4", 0: "ps6"}
            for b in (2, 0):
                mm(R(twin[b]), R("id1"), R(zs, 256 * b, 256 * b + 512), True, False)
            high(1)
            high(0)
            for b in (2, 0):
                partner(b)
                mm(R(twin[b]), R("id1"), R(lm, 256 * b, 256 * b + 512), False, False)
            for b in (3, 1):
                partner(b)
            for b in (2, 0):
                mm(R(twin[b]), R("idn"), R("ff", 512 * b, 512 * (b + 1)), False, True)
                act(mixed(b), R(twin[b]), bias=2561.0)
            pointers()
            high_half(R("q1"))
            for b in (3, 1):
                less(b)
            taken(True)
            parts = [("A", 0, 3), ("V", 8, 11), ("A", 3, 5), ("V", 11, 13), ("A", 5, 7), ("V", 13, 15), ("A", 7, 8), ("V", 15, 16)]
        else:
            pointers()
            high(1)
            partner(2)
            partner(3)
            less(2)
            partner(0)
            high(0)
            less(3)
            partner(1)
            less(0)
            less(1)
            parts = [("A", 0, 1), ("V", 8, 9), ("A", 1, 3), ("V", 9, 11), ("A", 3, 6), ("V", 11, 14), ("A", 6, 8), ("V", 14, 16)]
        dst, o = (store[c], MO) if more else ("outm", 0)
        for q, a, b in parts:
            out, src = R(dst, o + 256 * a, o + 256 * b), IND(R(cur), R("ptr", 16 * a, 16 * b))
            if q == "A":
                act(out, src)
            else:
                cp(out, src)
            if not more:
                dma("S", T.ym[:, 256 * a:256 * b], out)
        if more:
            sums(dst, [i for q, a, b in parts for i in range(a, b)], False)
            masks()

    for sem in sorted(total):
        if known["G"].get(sem, 0) < total[sem]:
            g.wait_ge(T.sem[sem], total[sem])
